import numpy as np
import ml_dtypes


def mxq(x, axis, fmt="e4m3"):
    dtype, down = {"e4m3": (ml_dtypes.float8_e4m3fn, 7), "e5m2": (ml_dtypes.float8_e5m2, 14)}[fmt]
    v = np.moveaxis(np.asarray(x, np.float32).astype(ml_dtypes.bfloat16).astype(np.float64), axis, -1)
    blocks = v.reshape(v.shape[:-1] + (-1, 32))
    amax = np.abs(blocks).max(-1, keepdims=True)
    byte = np.maximum(np.where(amax > 0, np.frexp(amax)[1] - 1 + 127, 0) - down, 1)
    scale = np.exp2(byte - 127.0)
    codes = (blocks / scale).astype(np.float32).astype(dtype).astype(np.float64)
    return np.moveaxis((codes * scale).reshape(v.shape), -1, axis)


WIDE = False


def mx_kscale(k):
    if not WIDE:
        return np.ones(k)
    levels = np.array([10, -10, 5, -5, 0])
    if k % 512:
        return np.exp2(np.random.permutation(np.resize(levels, k // 32))).repeat(32)
    a = np.empty((k // 512, 16))
    for p in range(k // 512):
        a[p, :8] = np.random.permutation(np.resize(levels, 8))
        for g in range(8):
            far = levels[np.abs(levels - a[p, g]) >= 10]
            a[p, g + 8] = far[np.random.randint(len(far))]
    return np.exp2(a.ravel()).repeat(32)


def f64(x):
    return np.asarray(x).astype(np.float64)


def striped(idx):
    return np.tile(idx.reshape(-1, 16).T, (8, 1)).astype(np.uint16)


def unstriped(offs):
    return offs[:16].T.reshape(-1).astype(np.int64)


def pack_weight(w):
    k, n = w.shape
    w = f64(np.asarray(w, np.float32).astype(ml_dtypes.bfloat16)).reshape(k // 32, 32, n)
    amax = np.abs(w).max(1)
    byte = np.clip(np.where(amax > 0, np.frexp(amax)[1] - 1 + 127 - 7, 1), 1, 254)
    scaled = (w * np.exp2(127.0 - byte)[:, None, :]).reshape(k, n).astype(np.float32)
    words = np.ascontiguousarray(scaled.reshape(k // 512, 128, 4, n).transpose(0, 1, 3, 2)).astype(ml_dtypes.float8_e4m3fn).view(np.uint8)
    return words, np.ascontiguousarray(byte.astype(np.uint8).reshape(k // 512, 16, n))


def unpack_weight(words, scales):
    g, p, n, _ = words.shape
    vals = np.ascontiguousarray(words).view(ml_dtypes.float8_e4m3fn).astype(np.float64) * np.repeat(np.exp2(scales.astype(np.float64) - 127.0), 8, axis=1)[..., None]
    return vals.transpose(0, 1, 3, 2).reshape(g * 512, n)


def sigmoid(v):
    return 1.0 / (1.0 + np.exp(-np.maximum(v, -700.0)))


K, T, S, H, C = 512, 2048, 256, 512, 512


def setup_inputs():
    n = np.random.standard_normal
    s = mx_kscale(K)[:, None]
    packed_xT = pack_weight(n((K, T)) * s)
    return {
        "x_words": packed_xT[0],
        "x_scales": packed_xT[1],
        "w1": (n((K, H)) / np.sqrt(K) / s).astype(np.float32),
        "w2": (n((K, H)) / np.sqrt(K) / s).astype(np.float32),
        "sl": np.random.uniform(1.0, 2.0, (H, 1)).astype(np.float32),
        "th": (0.5 * n((H, 1))).astype(np.float32),
        "gs": (np.random.uniform(0.5, 1.5, (K, 1)) / s).astype(np.float32),
        "sl2": np.random.uniform(1.0, 2.0, (C, 1)).astype(np.float32),
        "offs": striped(np.random.permutation(T)[:S]),
        "two": striped(np.random.permutation(T)[:S]),
        "n1": striped(np.random.permutation(S)),
        "n2": striped(np.random.permutation(S)),
        "cand": striped(np.random.permutation(T)[:C]),
        "n3": striped(np.random.permutation(S)),
    }


def reference(x_words, x_scales, w1, w2, sl, th, gs, sl2, offs, two, n1, n2, cand, n3):
    x_cand = unpack_weight(x_words, x_scales)[:, unstriped(cand)]
    xq = unpack_weight(x_words, x_scales)[:, unstriped(offs)]
    y = mxq(f64(w1), 0, "e4m3").T @ xq
    x_two = unpack_weight(x_words, x_scales)[:, unstriped(two)]
    d = mxq(f64(w2), 0, "e4m3").T @ x_two
    sg = sigmoid(f64(sl) * (d[:, unstriped(n1)] - f64(th)))
    z = f64(gs) * (np.maximum(y * sg, d[:, unstriped(n2)] - d))
    s = 0.0625 * ((x_cand.T @ mxq(z, 0, "e4m3")))
    mu = s.mean(axis=1, keepdims=True)
    sg2 = sigmoid(f64(sl2) * (s[:, unstriped(n3)] - mu))
    return (s - mu) * sg2

@@ -1,0 +1,167 @@
+from contextlib import ExitStack
+
+import concourse.mybir as mybir
+
+F32 = mybir.dt.float32
+BF16 = mybir.dt.bfloat16
+I32 = mybir.dt.int32
+U32 = mybir.dt.uint32
+U16 = mybir.dt.uint16
+U8 = mybir.dt.uint8
+FP8X4 = mybir.dt.float8_e4m3fn_x4
+ALU = mybir.AluOpType
+ACT = mybir.ActivationFunctionType
+
+P = 128
+PACK = 4
+K, T, S, H, C = 512, 2048, 256, 512, 512
+FLOPS = 2 * K * (H * S + H * S + C * S)
+
+
+def tile_picked_twcmxbecn_none_p_kernel(tc, x_words, x_scales, w1, w2, sl, th, gs, sl2, offs, two, n1, n2, cand, n3, out):
+    nc = tc.nc
+    with ExitStack() as ctx:
+        keep = ctx.enter_context(tc.tile_pool(name="keep", bufs=1))
+        psum = ctx.enter_context(tc.psum_pool(name="psum", bufs=1))
+
+        def sb(name, shape, dtype):
+            return keep.tile(shape, dtype, name=name, align_bytes=64)
+
+        def load_list(name, src):
+            tile = keep.tile(list(src.shape), U16, name=name)
+            nc.sync.dma_start(tile[:], src)
+            return tile
+
+        bytes_tab = sb("bytes_tab", [P, T], U8)
+        nc.vector.memset(bytes_tab[:].bitcast(I32), 0)
+        two_l = load_list("two_l", two)
+        offs_l = load_list("offs_l", offs)
+        cand_l = load_list("cand_l", cand)
+        for q, queue in enumerate((nc.sync, nc.scalar, nc.sync, nc.scalar)):
+            queue.dma_start(bytes_tab[32 * q : 32 * q + 4, :].bitcast(I32), x_scales[0, 4 * q : 4 * q + 4, :].bitcast(I32))
+        words_tab = sb("words_tab", [P, T], U32)
+        nc.sync.dma_start(words_tab[:].bitcast(I32), x_words[0].rearrange("p c r -> p (c r)").bitcast(I32))
+
+        half = H // 2
+        raw = {}
+        for name, w in (("w2", w2), ("w1", w1)):
+            for h in range(2):
+                raw[name, h] = sb("raw_%s_%d" % (name, h), [P, PACK, half], F32)
+                nc.sync.dma_start(raw[name, h][:], w.rearrange("(p j) c -> p j c", j=PACK)[:, :, h * half : (h + 1) * half])
+        n1_l = load_list("n1_l", n1)
+        n2_l = load_list("n2_l", n2)
+        n3_l = load_list("n3_l", n3)
+        sl_t = sb("sl_t", [P, PACK], F32)
+        th_t = sb("th_t", [P, PACK], F32)
+        gs_t = sb("gs_t", [P, PACK], F32)
+        sl2_t = sb("sl2_t", [P, C // P], F32)
+        for tile, src in ((sl_t, sl), (th_t, th), (gs_t, gs)):
+            nc.gpsimd.dma_start(tile[:], src.rearrange("(p t) o -> p (t o)", t=PACK))
+        with nc.allow_non_contiguous_dma(reason="one slope a partition and block"):
+            nc.gpsimd.dma_start(sl2_t[:], sl2.rearrange("(b p) o -> p (b o)", p=P))
+
+        bias1 = sb("bias1", [P, PACK], F32)
+        nc.gpsimd.tensor_tensor(bias1[:], sl_t[:], th_t[:], ALU.mult)
+        nc.gpsimd.tensor_scalar(bias1[:], bias1[:], -1.0, 0.0, ALU.mult, ALU.add)
+        coef = sb("coef", [P, C // P, 2], F32)
+        nc.gpsimd.memset(coef[:, :, 1], -1.0 / S)
+        nc.gpsimd.tensor_scalar(coef[:, :, 0], sl2_t[:], -1.0 / S, 0.0, ALU.mult, ALU.add)
+
+        picked = {}
+        for name, lst, n in (("two", two_l, S), ("offs", offs_l, S), ("cand", cand_l, C)):
+            picked[name] = (sb("words_" + name, [P, n], U32), sb("bytes_" + name, [P, n], U8), lst)
+
+        def gather_bytes(name):
+            nc.vector.tensor_copy(picked[name][1][:], bytes_tab[:].indirect(picked[name][2][:]))
+
+        def gather_words(name):
+            nc.vector.tensor_copy(picked[name][0][:], words_tab[:].indirect(picked[name][2][:]))
+
+        grouped = {name: sb("grouped_" + name, [P, PACK, P, PACK], BF16) for name in ("w2", "w1")}
+        codes = {name: (sb("codes_" + name, [P, H], U32), sb("scales_" + name, [P, H], U8)) for name in ("w2", "w1")}
+
+        def cast(name, h, lo, hi, copy):
+            m = h * (half // PACK)
+            copy(grouped[name][:, :, m + lo : m + hi, :].rearrange("p t m j -> p m j t"),
+                 raw[name, h][:].rearrange("p j (m t) -> p m j t", t=PACK)[:, lo:hi])
+
+        def quantize(name):
+            nc.vector.quantize_mx(out=codes[name][0][:].bitcast(FP8X4), scales=codes[name][1][:],
+                                  in_=grouped[name][:].rearrange("p t m j -> p (t m j)"))
+
+        def project(bank, t, name, tokens):
+            cols = slice(t * P, (t + 1) * P)
+            nc.tensor.matmul_mx(out=bank[:, t % 2, :], lhsT=codes[name][0][:, cols].bitcast(FP8X4), lhsT_scale=codes[name][1][:, cols],
+                                rhs=picked[tokens][0][:].bitcast(FP8X4), rhs_scale=picked[tokens][1][:], start=True, stop=True)
+
+        for name in ("two", "offs", "cand"):
+            gather_bytes(name)
+        for name in ("two", "offs", "cand"):
+            gather_words(name)
+        cast("w2", 0, 0, 64, nc.scalar.copy)
+        cast("w2", 1, 0, 64, nc.vector.tensor_copy)
+        quantize("w2")
+        d_bank = [psum.tile([P, 2, S], F32, name="d_bank%d" % u) for u in range(2)]
+        y_bank = [psum.tile([P, 2, S], F32, name="y_bank%d" % u) for u in range(2)]
+        for t in range(PACK):
+            project(d_bank[t // 2], t, "w2", "two")
+        cast("w1", 0, 0, 64, nc.scalar.copy)
+        d_row = [sb("d_row%d" % t, [P, S], F32) for t in range(PACK)]
+        d_copy = (nc.vector.tensor_copy, nc.vector.tensor_copy, nc.scalar.copy, nc.scalar.copy)
+        for t in range(2):
+            d_copy[t](d_row[t][:], d_bank[0][:, t, :])
+        cast("w1", 1, 0, 64, nc.vector.tensor_copy)
+        quantize("w1")
+        for t in range(PACK):
+            project(y_bank[t // 2], t, "w1", "offs")
+
+        gate = sb("gate", [P, PACK, S], F32)
+        diff = sb("diff", [P, PACK, S], F32)
+        best = sb("best", [P, PACK, S], F32)
+        z = sb("z", [P, S, PACK], BF16)
+        z_codes = sb("z_codes", [P, S], U32)
+        z_scales = sb("z_scales", [P, S], U8)
+        hs = S // 2
+        hl = hs // 16
+        for h in range(2):
+            js = slice(h * hs, (h + 1) * hs)
+            ls = slice(h * hl, (h + 1) * hl)
+            for u in range(2):
+                ts = slice(2 * u, 2 * u + 2)
+                if h == 0 and u == 1:
+                    for t in range(2, 4):
+                        d_copy[t](d_row[t][:], d_bank[1][:, t - 2, :])
+                for t in range(2 * u, 2 * u + 2):
+                    nc.scalar.activation(gate[:, t, js], d_row[t][:].indirect(n1_l[:, ls]), ACT.Sigmoid,
+                                         bias=bias1[:, t : t + 1], scale=sl_t[:, t : t + 1])
+                for t in range(2 * u, 2 * u + 2):
+                    nc.scalar.activation(diff[:, t, js], d_row[t][:].indirect(n2_l[:, ls]), ACT.Copy)
+                nc.vector.tensor_tensor(best[:, ts, js], y_bank[u][:, :, js], gate[:, ts, js], ALU.mult)
+                nc.vector.tensor_tensor(diff[:, ts, js], diff[:, ts, js], d_bank[u][:, :, js], ALU.subtract)
+            for u in range(2):
+                ts = slice(2 * u, 2 * u + 2)
+                nc.vector.tensor_tensor(best[:, ts, js], best[:, ts, js], diff[:, ts, js], ALU.max)
+            nc.vector.tensor_tensor(z[:, js, :].rearrange("p (c i) t -> p c t i", i=2), best[:, :, js].rearrange("p t (c i) -> p c t i", i=2),
+                                    gs_t[:].unsqueeze(1).unsqueeze(3).to_broadcast([P, hs // 2, PACK, 2]), ALU.mult)
+            nc.vector.quantize_mx(out=z_codes[:, js].bitcast(FP8X4), scales=z_scales[:, js], in_=z[:, js, :].rearrange("p s t -> p (s t)"))
+
+        blocks = C // P
+        total = sb("total", [P, blocks], F32)
+        shift = sb("shift", [P, blocks, 2], F32)
+        gate2 = sb("gate2", [P, blocks, S], F32)
+        res = sb("res", [P, blocks, S], F32)
+        score = []
+        for b in range(blocks):
+            cols = slice(b * P, (b + 1) * P)
+            s_bank = psum.tile([P, S], F32, name="s_bank%d" % b)
+            nc.tensor.matmul_mx(out=s_bank[:], lhsT=picked["cand"][0][:, cols].bitcast(FP8X4), lhsT_scale=picked["cand"][1][:, cols],
+                                rhs=z_codes[:].bitcast(FP8X4), rhs_scale=z_scales[:], start=True, stop=True)
+            score.append(sb("score%d" % b, [P, S], F32))
+            nc.vector.tensor_scalar(score[b][:], s_bank[:], 0.0625, None, ALU.mult, ALU.add, accum_out=total[:, b : b + 1])
+            nc.vector.tensor_scalar(shift[:, b, :], coef[:, b, :], total[:, b : b + 1], None, ALU.mult)
+            for h in range(2):
+                nc.scalar.activation(gate2[:, b, h * hs : (h + 1) * hs], score[b][:].indirect(n3_l[:, h * hl : (h + 1) * hl]), ACT.Sigmoid,
+                                     bias=shift[:, b, 0:1], scale=sl2_t[:, b : b + 1])
+        for b in range(blocks):
+            nc.vector.scalar_tensor_tensor(res[:, b, :], score[b][:], shift[:, b, 1:2], gate2[:, b, :], ALU.add, ALU.mult)
+            nc.sync.dma_start(out[b * P : (b + 1) * P, :], res[:, b, :])

@@ -20,16 +20,27 @@ FLOPS = 2 * K * (H * S + H * S + C * S)
 
 def tile_picked_twcmxbecn_none_p_kernel(tc, x_words, x_scales, w1, w2, sl, th, gs, sl2, offs, two, n1, n2, cand, n3, out):
     nc = tc.nc
+    blocks = C // P
     with ExitStack() as ctx:
         keep = ctx.enter_context(tc.tile_pool(name="keep", bufs=1))
         psum = ctx.enter_context(tc.psum_pool(name="psum", bufs=1))
 
-        def sb(name, shape, dtype):
-            return keep.tile(shape, dtype, name=name, align_bytes=64)
+        def sb(name, shape, dtype, tag=""):
+            return keep.tile(shape, dtype, name=name, tag=tag or name, align_bytes=64)
 
         def load_list(name, src):
             tile = keep.tile(list(src.shape), U16, name=name)
             nc.sync.dma_start(tile[:], src)
+            return tile
+
+        def load_weight(name, w):
+            tile = sb(name, [P, PACK, H], F32)
+            nc.sync.dma_start(tile[:], w.rearrange("(p j) c -> p j c", j=PACK))
+            return tile
+
+        def load_rows(name, src):
+            tile = sb(name, [P, PACK], F32)
+            nc.sync.dma_start(tile[:], src.rearrange("(p t) o -> p (t o)", t=PACK))
             return tile
 
         bytes_tab = sb("bytes_tab", [P, T], U8)
@@ -39,33 +50,24 @@ def tile_picked_twcmxbecn_none_p_kernel(tc, x_words, x_scales, w1, w2, sl, th, g
         cand_l = load_list("cand_l", cand)
         for q, queue in enumerate((nc.sync, nc.scalar, nc.sync, nc.scalar)):
             queue.dma_start(bytes_tab[32 * q : 32 * q + 4, :].bitcast(I32), x_scales[0, 4 * q : 4 * q + 4, :].bitcast(I32))
+        raw = {"w2": load_weight("raw_w2", w2)}
         words_tab = sb("words_tab", [P, T], U32)
         nc.sync.dma_start(words_tab[:].bitcast(I32), x_words[0].rearrange("p c r -> p (c r)").bitcast(I32))
-
-        half = H // 2
-        raw = {}
-        for name, w in (("w2", w2), ("w1", w1)):
-            for h in range(2):
-                raw[name, h] = sb("raw_%s_%d" % (name, h), [P, PACK, half], F32)
-                nc.sync.dma_start(raw[name, h][:], w.rearrange("(p j) c -> p j c", j=PACK)[:, :, h * half : (h + 1) * half])
         n1_l = load_list("n1_l", n1)
         n2_l = load_list("n2_l", n2)
+        sl_t = load_rows("sl_t", sl)
+        th_t = load_rows("th_t", th)
+        raw["w1"] = load_weight("raw_w1", w1)
+        gs_t = load_rows("gs_t", gs)
         n3_l = load_list("n3_l", n3)
-        sl_t = sb("sl_t", [P, PACK], F32)
-        th_t = sb("th_t", [P, PACK], F32)
-        gs_t = sb("gs_t", [P, PACK], F32)
-        sl2_t = sb("sl2_t", [P, C // P], F32)
-        for tile, src in ((sl_t, sl), (th_t, th), (gs_t, gs)):
-            nc.gpsimd.dma_start(tile[:], src.rearrange("(p t) o -> p (t o)", t=PACK))
+        sl2_t = sb("sl2_t", [P, blocks], F32)
         with nc.allow_non_contiguous_dma(reason="one slope a partition and block"):
-            nc.gpsimd.dma_start(sl2_t[:], sl2.rearrange("(b p) o -> p (b o)", p=P))
+            nc.sync.dma_start(sl2_t[:], sl2.rearrange("(b p) o -> p (b o)", p=P))
 
-        bias1 = sb("bias1", [P, PACK], F32)
-        nc.gpsimd.tensor_tensor(bias1[:], sl_t[:], th_t[:], ALU.mult)
-        nc.gpsimd.tensor_scalar(bias1[:], bias1[:], -1.0, 0.0, ALU.mult, ALU.add)
-        coef = sb("coef", [P, C // P, 2], F32)
-        nc.gpsimd.memset(coef[:, :, 1], -1.0 / S)
-        nc.gpsimd.tensor_scalar(coef[:, :, 0], sl2_t[:], -1.0 / S, 0.0, ALU.mult, ALU.add)
+        d_row = [sb("d_row%d" % t, [P, 2 * S], F32) for t in range(PACK)]
+        score = [sb("score%d" % b, [P, 2 * S], F32) for b in range(blocks)]
+        for window in d_row + score:
+            nc.vector.memset(window[:, S:], 0.0)
 
         picked = {}
         for name, lst, n in (("two", two_l, S), ("offs", offs_l, S), ("cand", cand_l, C)):
@@ -80,12 +82,10 @@ def tile_picked_twcmxbecn_none_p_kernel(tc, x_words, x_scales, w1, w2, sl, th, g
         grouped = {name: sb("grouped_" + name, [P, PACK, P, PACK], BF16) for name in ("w2", "w1")}
         codes = {name: (sb("codes_" + name, [P, H], U32), sb("scales_" + name, [P, H], U8)) for name in ("w2", "w1")}
 
-        def cast(name, h, lo, hi, copy):
-            m = h * (half // PACK)
-            copy(grouped[name][:, :, m + lo : m + hi, :].rearrange("p t m j -> p m j t"),
-                 raw[name, h][:].rearrange("p j (m t) -> p m j t", t=PACK)[:, lo:hi])
-
-        def quantize(name):
+        def quantize_weight(name, on_scalar):
+            for copy, ms in ((nc.scalar.copy, slice(0, on_scalar)), (nc.vector.tensor_copy, slice(on_scalar, P)))[(0 if on_scalar else 1) :]:
+                copy(grouped[name][:, :, ms, :].rearrange("p t m j -> p m j t"),
+                     raw[name][:].rearrange("p j (m t) -> p m j t", t=PACK)[:, ms])
             nc.vector.quantize_mx(out=codes[name][0][:].bitcast(FP8X4), scales=codes[name][1][:],
                                   in_=grouped[name][:].rearrange("p t m j -> p (t m j)"))
 
@@ -96,48 +96,51 @@ def tile_picked_twcmxbecn_none_p_kernel(tc, x_words, x_scales, w1, w2, sl, th, g
 
         for name in ("two", "offs", "cand"):
             gather_bytes(name)
-        for name in ("two", "offs", "cand"):
-            gather_words(name)
-        cast("w2", 0, 0, 64, nc.scalar.copy)
-        cast("w2", 1, 0, 64, nc.vector.tensor_copy)
-        quantize("w2")
+        quantize_weight("w2", 80)
+        gather_words("two")
         d_bank = [psum.tile([P, 2, S], F32, name="d_bank%d" % u) for u in range(2)]
         y_bank = [psum.tile([P, 2, S], F32, name="y_bank%d" % u) for u in range(2)]
         for t in range(PACK):
             project(d_bank[t // 2], t, "w2", "two")
-        cast("w1", 0, 0, 64, nc.scalar.copy)
-        d_row = [sb("d_row%d" % t, [P, S], F32) for t in range(PACK)]
-        d_copy = (nc.vector.tensor_copy, nc.vector.tensor_copy, nc.scalar.copy, nc.scalar.copy)
-        for t in range(2):
-            d_copy[t](d_row[t][:], d_bank[0][:, t, :])
-        cast("w1", 1, 0, 64, nc.vector.tensor_copy)
-        quantize("w1")
+        gather_words("offs")
+        d_copy = (nc.scalar.copy, nc.scalar.copy, nc.scalar.copy, nc.scalar.copy)
+        for t in range(PACK):
+            d_copy[t](d_row[t][:, :S], d_bank[t // 2][:, t % 2, :])
+        bias1 = sb("bias1", [P, PACK], F32)
+        nc.vector.scalar_tensor_tensor(bias1[:], sl_t[:], -1.0, th_t[:], ALU.mult, ALU.mult)
+        gather_words("cand")
+        quantize_weight("w1", 0)
         for t in range(PACK):
             project(y_bank[t // 2], t, "w1", "offs")
 
         gate = sb("gate", [P, PACK, S], F32)
-        diff = sb("diff", [P, PACK, S], F32)
+        moved = sb("moved", [P, PACK, S], F32)
+        diff = sb("diff", [P, PACK, S], F32, tag="grouped_w1")
         best = sb("best", [P, PACK, S], F32)
         z = sb("z", [P, S, PACK], BF16)
         z_codes = sb("z_codes", [P, S], U32)
         z_scales = sb("z_scales", [P, S], U8)
+        s_bank = [psum.tile([P, S], F32, name="s_bank%d" % b) for b in range(blocks)]
+        total = [sb("total%d" % h, [P, blocks], F32) for h in range(2)]
+        bias2 = sb("bias2", [P, blocks], F32)
+        neg_mu = sb("neg_mu", [P, blocks], F32)
+        gate2 = sb("gate2", [P, blocks, S], F32)
+        res = sb("res", [P, blocks, S], F32)
         hs = S // 2
         hl = hs // 16
-        for h in range(2):
-            js = slice(h * hs, (h + 1) * hs)
-            ls = slice(h * hl, (h + 1) * hl)
+        halves = [(slice(h * hs, (h + 1) * hs), slice(h * hl, (h + 1) * hl)) for h in range(2)]
+        for u in range(2):
+            ts = slice(2 * u, 2 * u + 2)
+            for t in range(2 * u, 2 * u + 2):
+                nc.scalar.activation(moved[:, t, :], d_row[t][:].indirect(n2_l[:]), ACT.Copy)
+            nc.vector.tensor_tensor(diff[:, ts, :], moved[:, ts, :], d_bank[u][:], ALU.subtract)
+        for js, ls in halves:
             for u in range(2):
                 ts = slice(2 * u, 2 * u + 2)
-                if h == 0 and u == 1:
-                    for t in range(2, 4):
-                        d_copy[t](d_row[t][:], d_bank[1][:, t - 2, :])
                 for t in range(2 * u, 2 * u + 2):
                     nc.scalar.activation(gate[:, t, js], d_row[t][:].indirect(n1_l[:, ls]), ACT.Sigmoid,
                                          bias=bias1[:, t : t + 1], scale=sl_t[:, t : t + 1])
-                for t in range(2 * u, 2 * u + 2):
-                    nc.scalar.activation(diff[:, t, js], d_row[t][:].indirect(n2_l[:, ls]), ACT.Copy)
                 nc.vector.tensor_tensor(best[:, ts, js], y_bank[u][:, :, js], gate[:, ts, js], ALU.mult)
-                nc.vector.tensor_tensor(diff[:, ts, js], diff[:, ts, js], d_bank[u][:, :, js], ALU.subtract)
             for u in range(2):
                 ts = slice(2 * u, 2 * u + 2)
                 nc.vector.tensor_tensor(best[:, ts, js], best[:, ts, js], diff[:, ts, js], ALU.max)
@@ -145,23 +148,25 @@ def tile_picked_twcmxbecn_none_p_kernel(tc, x_words, x_scales, w1, w2, sl, th, g
                                     gs_t[:].unsqueeze(1).unsqueeze(3).to_broadcast([P, hs // 2, PACK, 2]), ALU.mult)
             nc.vector.quantize_mx(out=z_codes[:, js].bitcast(FP8X4), scales=z_scales[:, js], in_=z[:, js, :].rearrange("p s t -> p (s t)"))
 
-        blocks = C // P
-        total = sb("total", [P, blocks], F32)
-        shift = sb("shift", [P, blocks, 2], F32)
-        gate2 = sb("gate2", [P, blocks, S], F32)
-        res = sb("res", [P, blocks, S], F32)
-        score = []
-        for b in range(blocks):
+        def score_block(b, js):
             cols = slice(b * P, (b + 1) * P)
-            s_bank = psum.tile([P, S], F32, name="s_bank%d" % b)
-            nc.tensor.matmul_mx(out=s_bank[:], lhsT=picked["cand"][0][:, cols].bitcast(FP8X4), lhsT_scale=picked["cand"][1][:, cols],
-                                rhs=z_codes[:].bitcast(FP8X4), rhs_scale=z_scales[:], start=True, stop=True)
-            score.append(sb("score%d" % b, [P, S], F32))
-            nc.vector.tensor_scalar(score[b][:], s_bank[:], 0.0625, None, ALU.mult, ALU.add, accum_out=total[:, b : b + 1])
-            nc.vector.tensor_scalar(shift[:, b, :], coef[:, b, :], total[:, b : b + 1], None, ALU.mult)
-            for h in range(2):
-                nc.scalar.activation(gate2[:, b, h * hs : (h + 1) * hs], score[b][:].indirect(n3_l[:, h * hl : (h + 1) * hl]), ACT.Sigmoid,
-                                     bias=shift[:, b, 0:1], scale=sl2_t[:, b : b + 1])
+            nc.tensor.matmul_mx(out=s_bank[b][:, js], lhsT=picked["cand"][0][:, cols].bitcast(FP8X4), lhsT_scale=picked["cand"][1][:, cols],
+                                rhs=z_codes[:, js].bitcast(FP8X4), rhs_scale=z_scales[:, js], start=True, stop=True)
+
+        pieces = [[(slice(0, S), slice(0, S // 16))]] * (blocks - 1) + [halves]
+        first, second = halves[0][0], halves[1][0]
         for b in range(blocks):
-            nc.vector.scalar_tensor_tensor(res[:, b, :], score[b][:], shift[:, b, 1:2], gate2[:, b, :], ALU.add, ALU.mult)
-            nc.sync.dma_start(out[b * P : (b + 1) * P, :], res[:, b, :])
+            score_block(b, first)
+            nc.scalar.activation(score[b][:, first], s_bank[b][:, first], ACT.Copy, scale=0.0625, accum_out=total[0][:, b : b + 1])
+        for b in range(blocks):
+            col = slice(b, b + 1)
+            score_block(b, second)
+            nc.vector.tensor_scalar(score[b][:, second], s_bank[b][:, second], 0.0625, total[0][:, col], ALU.mult, ALU.add, accum_out=total[1][:, col])
+            nc.vector.tensor_scalar(bias2[:, col], total[1][:, col], sl2_t[:, col], -1.0 / S, ALU.mult, ALU.mult)
+            for js, ls in pieces[b]:
+                nc.scalar.activation(gate2[:, b, js], score[b][:].indirect(n3_l[:, ls]), ACT.Sigmoid, bias=bias2[:, col], scale=sl2_t[:, col])
+        nc.vector.tensor_scalar(neg_mu[:], total[1][:], -1.0 / S, None, ALU.mult)
+        for b in range(blocks):
+            for js, ls in pieces[b]:
+                nc.vector.scalar_tensor_tensor(res[:, b, js], score[b][:, js], neg_mu[:, b : b + 1], gate2[:, b, js], ALU.add, ALU.mult)
+                nc.sync.dma_start(out[b * P : (b + 1) * P, js], res[:, b, js])

@@ -50,6 +50,9 @@ def tile_picked_twcmxbecn_none_p_kernel(tc, x_words, x_scales, w1, w2, sl, th, g
         cand_l = load_list("cand_l", cand)
         for q, queue in enumerate((nc.sync, nc.scalar, nc.sync, nc.scalar)):
             queue.dma_start(bytes_tab[32 * q : 32 * q + 4, :].bitcast(I32), x_scales[0, 4 * q : 4 * q + 4, :].bitcast(I32))
+        warm = sb("warm", [P, 2], F32)
+        nc.vector.memset(warm[:, 0:1], 0.0)
+        nc.scalar.activation(warm[:, 1:2], warm[:, 0:1], ACT.Sigmoid)
         raw = {"w2": load_weight("raw_w2", w2)}
         words_tab = sb("words_tab", [P, T], U32)
         nc.sync.dma_start(words_tab[:].bitcast(I32), x_words[0].rearrange("p c r -> p (c r)").bitcast(I32))

from contextlib import ExitStack

import concourse.mybir as mybir

F32 = mybir.dt.float32
BF16 = mybir.dt.bfloat16
I32 = mybir.dt.int32
U32 = mybir.dt.uint32
U16 = mybir.dt.uint16
U8 = mybir.dt.uint8
FP8X4 = mybir.dt.float8_e4m3fn_x4
ALU = mybir.AluOpType
ACT = mybir.ActivationFunctionType

P = 128
PACK = 4
K, T, S, H, C = 512, 2048, 256, 512, 512
FLOPS = 2 * K * (H * S + H * S + C * S)


def tile_picked_twcmxbecn_none_p_kernel(tc, x_words, x_scales, w1, w2, sl, th, gs, sl2, offs, two, n1, n2, cand, n3, out):
    nc = tc.nc
    blocks = C // P
    with ExitStack() as ctx:
        keep = ctx.enter_context(tc.tile_pool(name="keep", bufs=1))
        psum = ctx.enter_context(tc.psum_pool(name="psum", bufs=1))

        def sb(name, shape, dtype, tag=""):
            return keep.tile(shape, dtype, name=name, tag=tag or name, align_bytes=64)

        def load_list(name, src):
            tile = keep.tile(list(src.shape), U16, name=name)
            nc.sync.dma_start(tile[:], src)
            return tile

        def load_weight(name, w):
            tile = sb(name, [P, PACK, H], F32)
            nc.sync.dma_start(tile[:], w.rearrange("(p j) c -> p j c", j=PACK))
            return tile

        def load_rows(name, src):
            tile = sb(name, [P, PACK], F32)
            nc.sync.dma_start(tile[:], src.rearrange("(p t) o -> p (t o)", t=PACK))
            return tile

        bytes_tab = sb("bytes_tab", [P, T], U8)
        nc.vector.memset(bytes_tab[:].bitcast(I32), 0)
        two_l = load_list("two_l", two)
        offs_l = load_list("offs_l", offs)
        cand_l = load_list("cand_l", cand)
        for q, queue in enumerate((nc.sync, nc.scalar, nc.sync, nc.scalar)):
            queue.dma_start(bytes_tab[32 * q : 32 * q + 4, :].bitcast(I32), x_scales[0, 4 * q : 4 * q + 4, :].bitcast(I32))
        warm = sb("warm", [P, 2], F32)
        nc.vector.memset(warm[:, 0:1], 0.0)
        nc.scalar.activation(warm[:, 1:2], warm[:, 0:1], ACT.Sigmoid)
        raw = {"w2": load_weight("raw_w2", w2)}
        words_tab = sb("words_tab", [P, T], U32)
        nc.sync.dma_start(words_tab[:].bitcast(I32), x_words[0].rearrange("p c r -> p (c r)").bitcast(I32))
        n1_l = load_list("n1_l", n1)
        n2_l = load_list("n2_l", n2)
        sl_t = load_rows("sl_t", sl)
        th_t = load_rows("th_t", th)
        raw["w1"] = load_weight("raw_w1", w1)
        gs_t = load_rows("gs_t", gs)
        n3_l = load_list("n3_l", n3)
        sl2_t = sb("sl2_t", [P, blocks], F32)
        with nc.allow_non_contiguous_dma(reason="one slope a partition and block"):
            nc.sync.dma_start(sl2_t[:], sl2.rearrange("(b p) o -> p (b o)", p=P))

        d_row = [sb("d_row%d" % t, [P, 2 * S], F32) for t in range(PACK)]
        score = [sb("score%d" % b, [P, 2 * S], F32) for b in range(blocks)]
        for window in d_row + score:
            nc.vector.memset(window[:, S:], 0.0)

        picked = {}
        for name, lst, n in (("two", two_l, S), ("offs", offs_l, S), ("cand", cand_l, C)):
            picked[name] = (sb("words_" + name, [P, n], U32), sb("bytes_" + name, [P, n], U8), lst)

        def gather_bytes(name):
            nc.vector.tensor_copy(picked[name][1][:], bytes_tab[:].indirect(picked[name][2][:]))

        def gather_words(name):
            nc.vector.tensor_copy(picked[name][0][:], words_tab[:].indirect(picked[name][2][:]))

        grouped = {name: sb("grouped_" + name, [P, PACK, P, PACK], BF16) for name in ("w2", "w1")}
        codes = {name: (sb("codes_" + name, [P, H], U32), sb("scales_" + name, [P, H], U8)) for name in ("w2", "w1")}

        def quantize_weight(name, on_scalar):
            for copy, ms in ((nc.scalar.copy, slice(0, on_scalar)), (nc.vector.tensor_copy, slice(on_scalar, P)))[(0 if on_scalar else 1) :]:
                copy(grouped[name][:, :, ms, :].rearrange("p t m j -> p m j t"),
                     raw[name][:].rearrange("p j (m t) -> p m j t", t=PACK)[:, ms])
            nc.vector.quantize_mx(out=codes[name][0][:].bitcast(FP8X4), scales=codes[name][1][:],
                                  in_=grouped[name][:].rearrange("p t m j -> p (t m j)"))

        def project(bank, t, name, tokens):
            cols = slice(t * P, (t + 1) * P)
            nc.tensor.matmul_mx(out=bank[:, t % 2, :], lhsT=codes[name][0][:, cols].bitcast(FP8X4), lhsT_scale=codes[name][1][:, cols],
                                rhs=picked[tokens][0][:].bitcast(FP8X4), rhs_scale=picked[tokens][1][:], start=True, stop=True)

        for name in ("two", "offs", "cand"):
            gather_bytes(name)
        quantize_weight("w2", 80)
        gather_words("two")
        d_bank = [psum.tile([P, 2, S], F32, name="d_bank%d" % u) for u in range(2)]
        y_bank = [psum.tile([P, 2, S], F32, name="y_bank%d" % u) for u in range(2)]
        for t in range(PACK):
            project(d_bank[t // 2], t, "w2", "two")
        gather_words("offs")
        d_copy = (nc.scalar.copy, nc.scalar.copy, nc.scalar.copy, nc.scalar.copy)
        for t in range(PACK):
            d_copy[t](d_row[t][:, :S], d_bank[t // 2][:, t % 2, :])
        bias1 = sb("bias1", [P, PACK], F32)
        nc.vector.scalar_tensor_tensor(bias1[:], sl_t[:], -1.0, th_t[:], ALU.mult, ALU.mult)
        gather_words("cand")
        quantize_weight("w1", 0)
        for t in range(PACK):
            project(y_bank[t // 2], t, "w1", "offs")

        gate = sb("gate", [P, PACK, S], F32)
        moved = sb("moved", [P, PACK, S], F32)
        diff = sb("diff", [P, PACK, S], F32, tag="grouped_w1")
        best = sb("best", [P, PACK, S], F32)
        z = sb("z", [P, S, PACK], BF16)
        z_codes = sb("z_codes", [P, S], U32)
        z_scales = sb("z_scales", [P, S], U8)
        s_bank = [psum.tile([P, S], F32, name="s_bank%d" % b) for b in range(blocks)]
        total = [sb("total%d" % h, [P, blocks], F32) for h in range(2)]
        bias2 = sb("bias2", [P, blocks], F32)
        neg_mu = sb("neg_mu", [P, blocks], F32)
        gate2 = sb("gate2", [P, blocks, S], F32)
        res = sb("res", [P, blocks, S], F32)
        hs = S // 2
        hl = hs // 16
        halves = [(slice(h * hs, (h + 1) * hs), slice(h * hl, (h + 1) * hl)) for h in range(2)]
        for u in range(2):
            ts = slice(2 * u, 2 * u + 2)
            for t in range(2 * u, 2 * u + 2):
                nc.scalar.activation(moved[:, t, :], d_row[t][:].indirect(n2_l[:]), ACT.Copy)
            nc.vector.tensor_tensor(diff[:, ts, :], moved[:, ts, :], d_bank[u][:], ALU.subtract)
        for js, ls in halves:
            for u in range(2):
                ts = slice(2 * u, 2 * u + 2)
                for t in range(2 * u, 2 * u + 2):
                    nc.scalar.activation(gate[:, t, js], d_row[t][:].indirect(n1_l[:, ls]), ACT.Sigmoid,
                                         bias=bias1[:, t : t + 1], scale=sl_t[:, t : t + 1])
                nc.vector.tensor_tensor(best[:, ts, js], y_bank[u][:, :, js], gate[:, ts, js], ALU.mult)
            for u in range(2):
                ts = slice(2 * u, 2 * u + 2)
                nc.vector.tensor_tensor(best[:, ts, js], best[:, ts, js], diff[:, ts, js], ALU.max)
            nc.vector.tensor_tensor(z[:, js, :].rearrange("p (c i) t -> p c t i", i=2), best[:, :, js].rearrange("p t (c i) -> p c t i", i=2),
                                    gs_t[:].unsqueeze(1).unsqueeze(3).to_broadcast([P, hs // 2, PACK, 2]), ALU.mult)
            nc.vector.quantize_mx(out=z_codes[:, js].bitcast(FP8X4), scales=z_scales[:, js], in_=z[:, js, :].rearrange("p s t -> p (s t)"))

        def score_block(b, js):
            cols = slice(b * P, (b + 1) * P)
            nc.tensor.matmul_mx(out=s_bank[b][:, js], lhsT=picked["cand"][0][:, cols].bitcast(FP8X4), lhsT_scale=picked["cand"][1][:, cols],
                                rhs=z_codes[:, js].bitcast(FP8X4), rhs_scale=z_scales[:, js], start=True, stop=True)

        pieces = [[(slice(0, S), slice(0, S // 16))]] * (blocks - 1) + [halves]
        first, second = halves[0][0], halves[1][0]
        for b in range(blocks):
            score_block(b, first)
            nc.scalar.activation(score[b][:, first], s_bank[b][:, first], ACT.Copy, scale=0.0625, accum_out=total[0][:, b : b + 1])
        for b in range(blocks):
            col = slice(b, b + 1)
            score_block(b, second)
            nc.vector.tensor_scalar(score[b][:, second], s_bank[b][:, second], 0.0625, total[0][:, col], ALU.mult, ALU.add, accum_out=total[1][:, col])
            nc.vector.tensor_scalar(bias2[:, col], total[1][:, col], sl2_t[:, col], -1.0 / S, ALU.mult, ALU.mult)
            for js, ls in pieces[b]:
                nc.scalar.activation(gate2[:, b, js], score[b][:].indirect(n3_l[:, ls]), ACT.Sigmoid, bias=bias2[:, col], scale=sl2_t[:, col])
        nc.vector.tensor_scalar(neg_mu[:], total[1][:], -1.0 / S, None, ALU.mult)
        for b in range(blocks):
            for js, ls in pieces[b]:
                nc.vector.scalar_tensor_tensor(res[:, b, js], score[b][:, js], neg_mu[:, b : b + 1], gate2[:, b, js], ALU.add, ALU.mult)
                nc.sync.dma_start(out[b * P : (b + 1) * P, js], res[:, b, js])
